import numpy as np
import ml_dtypes


def mxq(x, axis, fmt="e4m3"):
    dtype, down = {"e4m3": (ml_dtypes.float8_e4m3fn, 7), "e5m2": (ml_dtypes.float8_e5m2, 14)}[fmt]
    v = np.moveaxis(np.asarray(x, np.float32).astype(ml_dtypes.bfloat16).astype(np.float64), axis, -1)
    blocks = v.reshape(v.shape[:-1] + (-1, 32))
    amax = np.abs(blocks).max(-1, keepdims=True)
    byte = np.maximum(np.where(amax > 0, np.frexp(amax)[1] - 1 + 127, 0) - down, 1)
    scale = np.exp2(byte - 127.0)
    codes = (blocks / scale).astype(np.float32).astype(dtype).astype(np.float64)
    return np.moveaxis((codes * scale).reshape(v.shape), -1, axis)


WIDE = False


def mx_kscale(k):
    if not WIDE:
        return np.ones(k)
    levels = np.array([10, -10, 5, -5, 0])
    if k % 512:
        return np.exp2(np.random.permutation(np.resize(levels, k // 32))).repeat(32)
    a = np.empty((k // 512, 16))
    for p in range(k // 512):
        a[p, :8] = np.random.permutation(np.resize(levels, 8))
        for g in range(8):
            far = levels[np.abs(levels - a[p, g]) >= 10]
            a[p, g + 8] = far[np.random.randint(len(far))]
    return np.exp2(a.ravel()).repeat(32)


def f64(x):
    return np.asarray(x).astype(np.float64)


def striped(idx):
    return np.tile(idx.reshape(-1, 16).T, (8, 1)).astype(np.uint16)


def unstriped(offs):
    return offs[:16].T.reshape(-1).astype(np.int64)


def pack_weight(w):
    k, n = w.shape
    w = f64(np.asarray(w, np.float32).astype(ml_dtypes.bfloat16)).reshape(k // 32, 32, n)
    amax = np.abs(w).max(1)
    byte = np.clip(np.where(amax > 0, np.frexp(amax)[1] - 1 + 127 - 7, 1), 1, 254)
    scaled = (w * np.exp2(127.0 - byte)[:, None, :]).reshape(k, n).astype(np.float32)
    words = np.ascontiguousarray(scaled.reshape(k // 512, 128, 4, n).transpose(0, 1, 3, 2)).astype(ml_dtypes.float8_e4m3fn).view(np.uint8)
    return words, np.ascontiguousarray(byte.astype(np.uint8).reshape(k // 512, 16, n))


def unpack_weight(words, scales):
    g, p, n, _ = words.shape
    vals = np.ascontiguousarray(words).view(ml_dtypes.float8_e4m3fn).astype(np.float64) * np.repeat(np.exp2(scales.astype(np.float64) - 127.0), 8, axis=1)[..., None]
    return vals.transpose(0, 1, 3, 2).reshape(g * 512, n)


K, T, S, N, U = 512, 1024, 512, 256, 512
P = 2 ** 7


def setup_inputs():
    n = np.random.standard_normal
    s = mx_kscale(K)[:, None]
    packed_xT = pack_weight(n((K, T)) * s)
    return {
        "x_words": packed_xT[0],
        "x_scales": packed_xT[1],
        "w1": (n((K, N)) / np.sqrt(K) / s).astype(np.float32),
        "one": (np.tile(np.random.uniform(0.85, 1.0, S), (P, 1))).astype(np.float32),
        "alpha": (np.random.uniform(0.3, 1.5, (N, 1))).astype(np.float32),
        "offs": striped(np.random.permutation(T)[:S]),
        "up": striped(np.random.randint(0, S, U)),
        "lo": striped(np.random.randint(0, S, U)),
    }


def reference(x_words, x_scales, w1, one, alpha, offs, up, lo):
    xq = unpack_weight(x_words, x_scales)[:, unstriped(offs)]
    y = mxq(f64(w1), 0, "e4m3").T @ xq
    suc = np.log(np.exp(y) + 1.0) + 0.1
    sat = f64(one)[:1] / (np.sqrt(f64(alpha) * ((suc) ** 2) + 1.0))
    cond = np.sqrt(sat) * ((-1.0 * (np.sqrt(-1.0 * ((sat) ** 2) + 1.001)) + 1.0) ** 2)
    ku = cond[:, unstriped(up)]
    kl = cond[:, unstriped(lo)]
    kf = 2.0 * ((ku * kl) / (ku + kl + 0.01))
    return 4.0 * (kf * (suc[:, unstriped(lo)] - suc[:, unstriped(up)] + 1.0))

@@ -1,0 +1,196 @@
+from contextlib import ExitStack
+
+import concourse.mybir as mybir
+
+F32 = mybir.dt.float32
+BF16 = mybir.dt.bfloat16
+U32 = mybir.dt.uint32
+I32 = mybir.dt.int32
+U16 = mybir.dt.uint16
+U8 = mybir.dt.uint8
+FP8X4 = mybir.dt.float8_e4m3fn_x4
+ACT = mybir.ActivationFunctionType
+ALU = mybir.AluOpType
+
+P = 128
+K, T, S, N, U = 512, 1024, 512, 256, 512
+PACK = 4
+TILES = N // P
+HALF = S // 2
+FLOPS = 2 * K * N * S
+
+
+def tile_picked_yrich_harm_p_kernel(
+    tc, x_words, x_scales, w1, one, alpha, offs, up, lo, out
+):
+    nc = tc.nc
+    with ExitStack() as ctx:
+        keep = ctx.enter_context(tc.tile_pool(name="keep", bufs=1))
+        psum = ctx.enter_context(tc.psum_pool(name="psum", bufs=1))
+
+        offs_t = keep.tile([P, S // 16], U16, name="offs_t")
+        up_t = keep.tile([P, U // 16], U16, name="up_t")
+        lo_t = keep.tile([P, U // 16], U16, name="lo_t")
+        xw = keep.tile([P, T], U32, name="xw", align_bytes=64)
+        xs = keep.tile([P, T], U8, name="xs", align_bytes=64)
+        one_t = keep.tile([P, S], F32, name="one_t")
+        alpha_t = keep.tile([P, TILES], F32, name="alpha_t")
+        floor = keep.tile([P, 1], F32, name="floor")
+        w_raw = keep.tile([P, PACK, N], F32, name="w_raw")
+
+        floor_in = keep.tile([P, 1], F32, name="floor_in")
+        nc.gpsimd.memset(xs[:].bitcast(I32), 0)
+        nc.sync.dma_start(offs_t[:], offs)
+        nc.sync.dma_start(w_raw[:], w1.rearrange("(p j) m -> p j m", j=PACK))
+        for q in range(4):
+            nc.sync.dma_start(
+                xs[32 * q : 32 * q + 4, :].bitcast(I32), x_scales[0, 4 * q : 4 * q + 4, :].bitcast(I32)
+            )
+        nc.sync.dma_start(xw[:].bitcast(I32), x_words[0].rearrange("p n t -> p (n t)").bitcast(I32))
+        nc.sync.dma_start(up_t[:], up)
+        nc.sync.dma_start(lo_t[:], lo)
+        with nc.allow_non_contiguous_dma(reason="one alpha a partition"):
+            nc.sync.dma_start(alpha_t[:], alpha.rearrange("(t p) o -> p (t o)", p=P))
+        nc.sync.dma_start(one_t[:], one)
+
+        nc.vector.memset(floor_in[:], -43.0)
+        nc.scalar.activation(floor[:], floor_in[:], ACT.Sigmoid)
+
+        w_bf = keep.tile([P, N, PACK], BF16, name="w_bf", align_bytes=64)
+        w_codes = keep.tile([P, N], U32, name="w_codes", align_bytes=64)
+        w_scales = keep.tile([P, N], U8, name="w_scales", align_bytes=64)
+        nc.scalar.copy(w_bf[:], w_raw[:].rearrange("p j m -> p m j"))
+
+        pw = [keep.tile([P, HALF], U32, name=f"pw{h}", align_bytes=64) for h in range(2)]
+        ps = keep.tile([P, S], U8, name="ps", align_bytes=64)
+        nc.vector.tensor_copy(ps[:], xs[:].indirect(offs_t[:]))
+        nc.vector.quantize_mx(
+            out=w_codes[:].bitcast(FP8X4), scales=w_scales[:], in_=w_bf[:].rearrange("p m j -> p (m j)")
+        )
+        for h in range(2):
+            nc.vector.tensor_copy(pw[h][:], xw[:].indirect(offs_t[:, 16 * h : 16 * h + 16]))
+
+        y = [psum.tile([P, TILES, HALF], F32, name=f"y{h}") for h in range(2)]
+        sig = keep.tile([P, TILES, S], F32, name="sig")
+        for h in range(2):
+            for t in range(TILES):
+                nc.tensor.matmul_mx(
+                    out=y[h][:, t, :],
+                    lhsT=w_codes[:, t * P : (t + 1) * P].bitcast(FP8X4),
+                    lhsT_scale=w_scales[:, t * P : (t + 1) * P],
+                    rhs=pw[h][:].bitcast(FP8X4),
+                    rhs_scale=ps[:, h * HALF : (h + 1) * HALF],
+                    start=True,
+                    stop=True,
+                )
+            nc.scalar.activation(sig[:, :, h * HALF : (h + 1) * HALF], y[h][:], ACT.Sigmoid, scale=-1.0)
+
+        spw = [keep.tile([P, 2 * S], F32, name=f"spw{t}") for t in range(TILES)]
+        aw = [keep.tile([P, 2 * S], F32, name=f"aw{t}") for t in range(TILES)]
+
+        def f32_tiles(name):
+            return [keep.tile([P, S], F32, name=f"{name}{t}") for t in range(TILES)]
+
+        q, rs, sat, z, rx, nw, u2, u4, c2 = [f32_tiles(n) for n in ("q", "rs", "sat", "z", "rx", "nw", "u2", "u4", "c2")]
+        su, d, au, r, r2, o = [f32_tiles(n) for n in ("su", "d", "au", "r", "r2", "o")]
+        RS = ACT.Abs_reciprocal_sqrt
+        A, B, W = (0, HALF), (HALF, S), (0, S)
+
+        def sl(tile, c, base=0):
+            return tile[:, base + c[0] : base + c[1]]
+
+        def lst(tile, c):
+            return tile[:, c[0] // 16 : c[1] // 16]
+
+        def f_ln(t, c):
+            nc.scalar.activation(sl(spw[t], c, S), sig[:, t, c[0] : c[1]], ACT.Ln, bias=floor[:])
+
+        def f_max(t, h):
+            c = (h * HALF, (h + 1) * HALF)
+            nc.vector.scalar_tensor_tensor(sl(spw[t], c), sl(spw[t], c, S), -1.0, y[h][:, t, :], ALU.mult, ALU.max)
+
+        def f_q(t, c):
+            nc.scalar.activation(sl(q[t], c), sl(spw[t], c), ACT.Square, bias=0.1)
+
+        def f_rs(t, c):
+            nc.scalar.activation(sl(rs[t], c), sl(q[t], c), RS, bias=1.0, scale=alpha_t[:, t : t + 1])
+
+        def f_sat(t, c):
+            nc.vector.tensor_tensor(sl(sat[t], c), sl(rs[t], c), sl(one_t, c), ALU.mult)
+
+        def f_z(t, c):
+            nc.scalar.activation(sl(z[t], c), sl(sat[t], c), ACT.Square)
+
+        def f_rx(t, c):
+            nc.scalar.activation(sl(rx[t], c), sl(z[t], c), RS, bias=1.001, scale=-1.0)
+
+        def f_nw(t, c):
+            nc.vector.scalar_tensor_tensor(sl(nw[t], c), sl(z[t], c), -1.001, sl(rx[t], c), ALU.add, ALU.mult)
+
+        def f_u2(t, c):
+            nc.scalar.activation(sl(u2[t], c), sl(nw[t], c), ACT.Square, bias=1.0)
+
+        def f_u4(t, c):
+            nc.scalar.activation(sl(u4[t], c), sl(u2[t], c), ACT.Square)
+
+        def f_c2(t, c):
+            nc.vector.tensor_tensor(sl(c2[t], c), sl(u4[t], c), sl(sat[t], c), ALU.mult)
+
+        def f_a(t, c):
+            nc.scalar.activation(sl(aw[t], c, S), sl(c2[t], c), RS, bias=1e-30, scale=1e4)
+
+        def f_A(t, c):
+            nc.scalar.activation(sl(aw[t], c), sl(aw[t], c, S), ACT.Identity, bias=1.0)
+
+        def f_su(t, c, dst):
+            nc.vector.tensor_copy(dst, spw[t][:].indirect(lst(up_t, c)))
+
+        def f_d(t, c, dst, src):
+            nc.vector.tensor_tensor(dst, spw[t][:].indirect(lst(lo_t, c)), src, ALU.subtract)
+
+        def f_au(t, c):
+            nc.vector.tensor_copy(sl(au[t], c), aw[t][:].indirect(lst(up_t, c)))
+
+        def f_ab(t, c):
+            nc.vector.tensor_tensor(sl(u2[1 - t], c), aw[t][:].indirect(lst(lo_t, c)), sl(au[t], c), ALU.mult)
+
+        def f_r(t, c):
+            nc.scalar.activation(sl(r[t], c), sl(u2[1 - t], c), RS, bias=-12.5, scale=12.5)
+
+        def f_r2(t, c):
+            nc.scalar.activation(sl(r2[t], c), sl(r[t], c), ACT.Square)
+
+        def f_o(t, c, dsrc):
+            nc.vector.scalar_tensor_tensor(sl(o[t], c), dsrc, 1.0, sl(r2[t], c), ALU.add, ALU.mult)
+            nc.sync.dma_start(out[t * P : (t + 1) * P, c[0] : c[1]], sl(o[t], c))
+
+        C, E = (256, 384), (384, 512)
+        f_ln(0, A); f_ln(0, B); f_ln(1, W)
+        f_max(0, 0); f_max(0, 1); f_max(1, 0); f_max(1, 1)
+        f_q(0, A); f_q(0, B)
+        f_su(0, W, su[0][:])
+        f_d(0, W, d[0][:], su[0][:])
+        f_rs(0, A); f_rs(0, B); f_q(1, W); f_rs(1, W)
+        f_sat(0, A); f_sat(0, B)
+        f_su(1, A, sl(q[0], B))
+        f_sat(1, W)
+        f_z(0, A); f_z(0, B); f_rx(0, A); f_rx(0, B); f_z(1, W)
+        f_nw(0, A); f_nw(0, B)
+        f_su(1, B, sl(rx[0], A))
+        f_d(1, A, sl(z[0], A), sl(q[0], B))
+        f_u2(0, A); f_u2(0, B); f_u4(0, A); f_u4(0, B); f_rx(1, W)
+        f_c2(0, A); f_c2(0, B)
+        f_nw(1, W)
+        f_a(0, A); f_a(0, B); f_A(0, A); f_A(0, B)
+        f_d(1, B, sl(c2[0], A), sl(rx[0], A))
+        f_u2(1, A); f_u2(1, B); f_u4(1, A); f_u4(1, B)
+        f_au(0, W)
+        f_c2(1, A); f_c2(1, B)
+        f_ab(0, W)
+        f_a(1, A); f_a(1, B); f_A(1, A); f_A(1, B)
+        f_r(0, W); f_r2(0, W)
+        f_au(1, W)
+        f_ab(1, A); f_ab(1, C); f_ab(1, E)
+        f_o(0, W, d[0][:])
+        f_r(1, A); f_r2(1, A); f_r(1, C); f_r(1, E); f_r2(1, C); f_r2(1, E)
+        f_o(1, A, sl(z[0], A)); f_o(1, C, c2[0][:, 0:128]); f_o(1, E, c2[0][:, 128:256])

@@ -33,164 +33,181 @@ def tile_picked_yrich_harm_p_kernel(
         lo_t = keep.tile([P, U // 16], U16, name="lo_t")
         xw = keep.tile([P, T], U32, name="xw", align_bytes=64)
         xs = keep.tile([P, T], U8, name="xs", align_bytes=64)
-        one_t = keep.tile([P, S], F32, name="one_t")
-        alpha_t = keep.tile([P, TILES], F32, name="alpha_t")
         floor = keep.tile([P, 1], F32, name="floor")
-        w_raw = keep.tile([P, PACK, N], F32, name="w_raw")
-
         floor_in = keep.tile([P, 1], F32, name="floor_in")
-        nc.gpsimd.memset(xs[:].bitcast(I32), 0)
+        stage = keep.tile([P, PACK * N], F32, name="stage")
+
+        nc.vector.memset(xs[:].bitcast(I32), 0)
         nc.sync.dma_start(offs_t[:], offs)
-        nc.sync.dma_start(w_raw[:], w1.rearrange("(p j) m -> p j m", j=PACK))
+        nc.sync.dma_start(xw[:].bitcast(I32), x_words[0].rearrange("p n t -> p (n t)").bitcast(I32))
+        nc.sync.dma_start(stage[:], w1.rearrange("(p j) m -> p (j m)", j=PACK))
         for q in range(4):
-            nc.sync.dma_start(
+            nc.scalar.dma_start(
                 xs[32 * q : 32 * q + 4, :].bitcast(I32), x_scales[0, 4 * q : 4 * q + 4, :].bitcast(I32)
             )
-        nc.sync.dma_start(xw[:].bitcast(I32), x_words[0].rearrange("p n t -> p (n t)").bitcast(I32))
         nc.sync.dma_start(up_t[:], up)
         nc.sync.dma_start(lo_t[:], lo)
-        with nc.allow_non_contiguous_dma(reason="one alpha a partition"):
-            nc.sync.dma_start(alpha_t[:], alpha.rearrange("(t p) o -> p (t o)", p=P))
-        nc.sync.dma_start(one_t[:], one)
 
         nc.vector.memset(floor_in[:], -43.0)
         nc.scalar.activation(floor[:], floor_in[:], ACT.Sigmoid)
 
-        w_bf = keep.tile([P, N, PACK], BF16, name="w_bf", align_bytes=64)
-        w_codes = keep.tile([P, N], U32, name="w_codes", align_bytes=64)
-        w_scales = keep.tile([P, N], U8, name="w_scales", align_bytes=64)
-        nc.scalar.copy(w_bf[:], w_raw[:].rearrange("p j m -> p m j"))
-
-        pw = [keep.tile([P, HALF], U32, name=f"pw{h}", align_bytes=64) for h in range(2)]
+        pw = keep.tile([P, S], U32, name="pw", align_bytes=64)
         ps = keep.tile([P, S], U8, name="ps", align_bytes=64)
+        nc.vector.tensor_copy(pw[:], xw[:].indirect(offs_t[:]))
         nc.vector.tensor_copy(ps[:], xs[:].indirect(offs_t[:]))
-        nc.vector.quantize_mx(
-            out=w_codes[:].bitcast(FP8X4), scales=w_scales[:], in_=w_bf[:].rearrange("p m j -> p (m j)")
-        )
-        for h in range(2):
-            nc.vector.tensor_copy(pw[h][:], xw[:].indirect(offs_t[:, 16 * h : 16 * h + 16]))
-
-        y = [psum.tile([P, TILES, HALF], F32, name=f"y{h}") for h in range(2)]
-        sig = keep.tile([P, TILES, S], F32, name="sig")
-        for h in range(2):
-            for t in range(TILES):
-                nc.tensor.matmul_mx(
-                    out=y[h][:, t, :],
-                    lhsT=w_codes[:, t * P : (t + 1) * P].bitcast(FP8X4),
-                    lhsT_scale=w_scales[:, t * P : (t + 1) * P],
-                    rhs=pw[h][:].bitcast(FP8X4),
-                    rhs_scale=ps[:, h * HALF : (h + 1) * HALF],
-                    start=True,
-                    stop=True,
-                )
-            nc.scalar.activation(sig[:, :, h * HALF : (h + 1) * HALF], y[h][:], ACT.Sigmoid, scale=-1.0)
 
         spw = [keep.tile([P, 2 * S], F32, name=f"spw{t}") for t in range(TILES)]
+        sig1 = keep.tile([P, S], F32, name="sig1")
+        sig = [spw[1][:, S:], sig1[:]]
+        y = [psum.tile([P, S], F32, name=f"y{t}") for t in range(TILES)]
+        w_rows = stage[:].rearrange("p (j m) -> p j m", j=PACK)
+        for t in (1, 0):
+            w_bf = keep.tile([P, P, PACK], BF16, name=f"w_bf{t}", align_bytes=64)
+            w_codes = keep.tile([P, P], U32, name=f"w_codes{t}", align_bytes=64)
+            w_scales = keep.tile([P, P], U8, name=f"w_scales{t}", align_bytes=64)
+            nc.scalar.copy(w_bf[:], w_rows[:, :, t * P : (t + 1) * P].rearrange("p j m -> p m j"))
+            nc.vector.quantize_mx(
+                out=w_codes[:].bitcast(FP8X4), scales=w_scales[:], in_=w_bf[:].rearrange("p m j -> p (m j)")
+            )
+            nc.tensor.matmul_mx(
+                out=y[t][:],
+                lhsT=w_codes[:].bitcast(FP8X4),
+                lhsT_scale=w_scales[:],
+                rhs=pw[:].bitcast(FP8X4),
+                rhs_scale=ps[:],
+                start=True,
+                stop=True,
+            )
+        for t in (1, 0):
+            nc.scalar.activation(sig[t], y[t][:], ACT.Sigmoid, scale=-1.0)
+        one_t = stage[:, 0:S]
+        alpha_t = stage[:, S : S + TILES]
+        with nc.allow_non_contiguous_dma(reason="one alpha a partition"):
+            nc.sync.dma_start(alpha_t, alpha.rearrange("(t p) o -> p (t o)", p=P))
+        nc.sync.dma_start(one_t, one)
+
         aw = [keep.tile([P, 2 * S], F32, name=f"aw{t}") for t in range(TILES)]
-
-        def f32_tiles(name):
-            return [keep.tile([P, S], F32, name=f"{name}{t}") for t in range(TILES)]
-
-        q, rs, sat, z, rx, nw, u2, u4, c2 = [f32_tiles(n) for n in ("q", "rs", "sat", "z", "rx", "nw", "u2", "u4", "c2")]
-        su, d, au, r, r2, o = [f32_tiles(n) for n in ("su", "d", "au", "r", "r2", "o")]
         RS = ACT.Abs_reciprocal_sqrt
         A, B, W = (0, HALF), (HALF, S), (0, S)
+        C, E = (256, 384), (384, 512)
 
-        def sl(tile, c, base=0):
-            return tile[:, base + c[0] : base + c[1]]
+        def buf(name, n=S):
+            return keep.tile([P, n], F32, name=name)[:]
+
+        def sl(ap, c, base=0):
+            return ap[:, base + c[0] : base + c[1]]
 
         def lst(tile, c):
             return tile[:, c[0] // 16 : c[1] // 16]
 
-        def f_ln(t, c):
-            nc.scalar.activation(sl(spw[t], c, S), sig[:, t, c[0] : c[1]], ACT.Ln, bias=floor[:])
+        def act(dst, src, func, **kw):
+            nc.scalar.activation(dst, src, func, **kw)
 
-        def f_max(t, h):
-            c = (h * HALF, (h + 1) * HALF)
-            nc.vector.scalar_tensor_tensor(sl(spw[t], c), sl(spw[t], c, S), -1.0, y[h][:, t, :], ALU.mult, ALU.max)
+        def f_ln(t, c):
+            act(sl(spw[t], c, S), sl(sig[t], c), ACT.Ln, bias=floor[:])
+
+        def f_max(t, c):
+            nc.vector.scalar_tensor_tensor(sl(spw[t], c), sl(spw[t], c, S), -1.0, sl(y[t], c), ALU.mult, ALU.max)
 
         def f_q(t, c):
-            nc.scalar.activation(sl(q[t], c), sl(spw[t], c), ACT.Square, bias=0.1)
+            act(sl(q[t], c), sl(spw[t], c), ACT.Square, bias=0.1)
 
         def f_rs(t, c):
-            nc.scalar.activation(sl(rs[t], c), sl(q[t], c), RS, bias=1.0, scale=alpha_t[:, t : t + 1])
+            act(sl(rs[t], c), sl(q[t], c), RS, bias=1.0, scale=alpha_t[:, t : t + 1])
 
         def f_sat(t, c):
             nc.vector.tensor_tensor(sl(sat[t], c), sl(rs[t], c), sl(one_t, c), ALU.mult)
 
         def f_z(t, c):
-            nc.scalar.activation(sl(z[t], c), sl(sat[t], c), ACT.Square)
+            act(sl(z[t], c), sl(sat[t], c), ACT.Square)
 
         def f_rx(t, c):
-            nc.scalar.activation(sl(rx[t], c), sl(z[t], c), RS, bias=1.001, scale=-1.0)
+            act(sl(rx[t], c), sl(z[t], c), RS, bias=1.001, scale=-1.0)
 
         def f_nw(t, c):
             nc.vector.scalar_tensor_tensor(sl(nw[t], c), sl(z[t], c), -1.001, sl(rx[t], c), ALU.add, ALU.mult)
 
         def f_u2(t, c):
-            nc.scalar.activation(sl(u2[t], c), sl(nw[t], c), ACT.Square, bias=1.0)
+            act(sl(u2[t], c), sl(nw[t], c), ACT.Square, bias=1.0)
 
         def f_u4(t, c):
-            nc.scalar.activation(sl(u4[t], c), sl(u2[t], c), ACT.Square)
+            act(sl(u4[t], c), sl(u2[t], c), ACT.Square)
 
         def f_c2(t, c):
             nc.vector.tensor_tensor(sl(c2[t], c), sl(u4[t], c), sl(sat[t], c), ALU.mult)
 
         def f_a(t, c):
-            nc.scalar.activation(sl(aw[t], c, S), sl(c2[t], c), RS, bias=1e-30, scale=1e4)
+            act(sl(aw[t], c, S), sl(c2[t], c), RS, bias=1e-30, scale=1e4)
 
         def f_A(t, c):
-            nc.scalar.activation(sl(aw[t], c), sl(aw[t], c, S), ACT.Identity, bias=1.0)
+            act(sl(aw[t], c), sl(aw[t], c, S), ACT.Identity, bias=1.0)
 
-        def f_su(t, c, dst):
-            nc.vector.tensor_copy(dst, spw[t][:].indirect(lst(up_t, c)))
+        def f_su(t, c):
+            nc.vector.tensor_copy(sl(su[t], c), spw[t][:].indirect(lst(up_t, c)))
 
-        def f_d(t, c, dst, src):
-            nc.vector.tensor_tensor(dst, spw[t][:].indirect(lst(lo_t, c)), src, ALU.subtract)
+        def f_d(t, c):
+            nc.vector.tensor_tensor(sl(d[t], c), spw[t][:].indirect(lst(lo_t, c)), sl(su[t], c), ALU.subtract)
 
         def f_au(t, c):
             nc.vector.tensor_copy(sl(au[t], c), aw[t][:].indirect(lst(up_t, c)))
 
         def f_ab(t, c):
-            nc.vector.tensor_tensor(sl(u2[1 - t], c), aw[t][:].indirect(lst(lo_t, c)), sl(au[t], c), ALU.mult)
+            nc.vector.tensor_tensor(sl(ab[t], c), aw[t][:].indirect(lst(lo_t, c)), sl(au[t], c), ALU.mult)
 
         def f_r(t, c):
-            nc.scalar.activation(sl(r[t], c), sl(u2[1 - t], c), RS, bias=-12.5, scale=12.5)
+            act(sl(r[t], c), sl(ab[t], c), RS, bias=-12.5, scale=12.5)
 
         def f_r2(t, c):
-            nc.scalar.activation(sl(r2[t], c), sl(r[t], c), ACT.Square)
+            act(sl(r2[t], c), sl(r[t], c), ACT.Square)
 
-        def f_o(t, c, dsrc):
-            nc.vector.scalar_tensor_tensor(sl(o[t], c), dsrc, 1.0, sl(r2[t], c), ALU.add, ALU.mult)
+        def f_o(t, c):
+            nc.vector.scalar_tensor_tensor(sl(o[t], c), sl(d[t], c), 1.0, sl(r2[t], c), ALU.add, ALU.mult)
             nc.sync.dma_start(out[t * P : (t + 1) * P, c[0] : c[1]], sl(o[t], c))
 
-        C, E = (256, 384), (384, 512)
-        f_ln(0, A); f_ln(0, B); f_ln(1, W)
-        f_max(0, 0); f_max(0, 1); f_max(1, 0); f_max(1, 1)
+        rs, sat, nw, u4, ab, r, r2, o, z, q, rx, u2, c2, su, d, au = [[buf(f"{n}{t}") for t in range(TILES)] for n in ("rs", "sat", "nw", "u4", "ab", "r", "r2", "o", "z", "q", "rx", "u2", "c2", "su", "d", "au")]
+
+        t1 = buf("d0_q0_su1_z0", 1408)
+        d[0] = t1[:, 0:512]
+        q[0] = t1[:, 256:768]
+        su[1] = t1[:, 640:1152]
+        z[0] = t1[:, 896:1408]
+        t3 = buf("c20_d1_ab1", 1024)
+        c2[0] = t3[:, 0:512]
+        d[1] = t3[:, 256:768]
+        ab[1] = t3[:, 512:1024]
+        ab[0] = u2[1]
+        t5 = buf("c21_r0", 768)
+        c2[1] = t5[:, 0:512]
+        r[0] = t5[:, 256:768]
+
+        f_ln(0, A); f_ln(0, B); f_ln(1, A); f_ln(1, B)
+        f_max(0, A); f_max(0, B)
         f_q(0, A); f_q(0, B)
-        f_su(0, W, su[0][:])
-        f_d(0, W, d[0][:], su[0][:])
+        f_su(0, W)
+        f_max(1, A); f_max(1, B)
         f_rs(0, A); f_rs(0, B); f_q(1, W); f_rs(1, W)
+        f_d(0, A)
         f_sat(0, A); f_sat(0, B)
-        f_su(1, A, sl(q[0], B))
+        f_d(0, B)
+        f_su(1, (0, 128))
         f_sat(1, W)
         f_z(0, A); f_z(0, B); f_rx(0, A); f_rx(0, B); f_z(1, W)
         f_nw(0, A); f_nw(0, B)
-        f_su(1, B, sl(rx[0], A))
-        f_d(1, A, sl(z[0], A), sl(q[0], B))
+        f_su(1, (128, 512))
         f_u2(0, A); f_u2(0, B); f_u4(0, A); f_u4(0, B); f_rx(1, W)
         f_c2(0, A); f_c2(0, B)
         f_nw(1, W)
         f_a(0, A); f_a(0, B); f_A(0, A); f_A(0, B)
-        f_d(1, B, sl(c2[0], A), sl(rx[0], A))
+        f_d(1, A)
         f_u2(1, A); f_u2(1, B); f_u4(1, A); f_u4(1, B)
         f_au(0, W)
         f_c2(1, A); f_c2(1, B)
         f_ab(0, W)
         f_a(1, A); f_a(1, B); f_A(1, A); f_A(1, B)
         f_r(0, W); f_r2(0, W)
-        f_au(1, W)
-        f_ab(1, A); f_ab(1, C); f_ab(1, E)
-        f_o(0, W, d[0][:])
-        f_r(1, A); f_r2(1, A); f_r(1, C); f_r(1, E); f_r2(1, C); f_r2(1, E)
-        f_o(1, A, sl(z[0], A)); f_o(1, C, c2[0][:, 0:128]); f_o(1, E, c2[0][:, 128:256])
+        f_au(1, A); f_au(1, B)
+        f_ab(1, A); f_ab(1, B)
+        f_o(0, W)
+        f_r(1, A); f_r2(1, A); f_r(1, B); f_r2(1, B)
+        f_d(1, B)
+        f_o(1, A); f_o(1, B)

@@ -13,11 +13,17 @@ ACT = mybir.ActivationFunctionType
 ALU = mybir.AluOpType
 
 P = 128
-K, T, S, N, U = 512, 1024, 512, 256, 512
+K, T, N = 512, 1024, 256
+S = 512
 PACK = 4
-TILES = N // P
+LIST_ROWS = 16
 HALF = S // 2
+LEAD, TRAIL = 0, 1
 FLOPS = 2 * K * N * S
+
+FIRST, SECOND, WHOLE = (0, HALF), (HALF, S), (0, S)
+HALVES = (FIRST, SECOND)
+PIECE = 128
 
 
 def tile_picked_yrich_harm_p_kernel(
@@ -28,186 +34,211 @@ def tile_picked_yrich_harm_p_kernel(
         keep = ctx.enter_context(tc.tile_pool(name="keep", bufs=1))
         psum = ctx.enter_context(tc.psum_pool(name="psum", bufs=1))
 
-        offs_t = keep.tile([P, S // 16], U16, name="offs_t")
-        up_t = keep.tile([P, U // 16], U16, name="up_t")
-        lo_t = keep.tile([P, U // 16], U16, name="lo_t")
-        xw = keep.tile([P, T], U32, name="xw", align_bytes=64)
-        xs = keep.tile([P, T], U8, name="xs", align_bytes=64)
-        floor = keep.tile([P, 1], F32, name="floor")
-        floor_in = keep.tile([P, 1], F32, name="floor_in")
-        stage = keep.tile([P, PACK * N], F32, name="stage")
+        def floats(name, width=S):
+            return keep.tile([P, width], F32, name=name)[:]
 
-        nc.vector.memset(xs[:].bitcast(I32), 0)
+        def cols(ap, c):
+            return ap[:, c[0] : c[1]]
+
+        def entries(list_tile, c):
+            return list_tile[:, c[0] // LIST_ROWS : c[1] // LIST_ROWS]
+
+        offs_t = keep.tile([P, S // LIST_ROWS], U16, name="offs_t")
+        up_t = keep.tile([P, S // LIST_ROWS], U16, name="up_t")
+        lo_t = keep.tile([P, S // LIST_ROWS], U16, name="lo_t")
+        table_words = keep.tile([P, T], U32, name="table_words", align_bytes=64)
+        table_scales = keep.tile([P, T], U8, name="table_scales", align_bytes=64)
+        stage = floats("stage", PACK * N)
+
+        nc.vector.memset(table_scales[:].bitcast(I32), 0)
         nc.sync.dma_start(offs_t[:], offs)
-        nc.sync.dma_start(xw[:].bitcast(I32), x_words[0].rearrange("p n t -> p (n t)").bitcast(I32))
-        nc.sync.dma_start(stage[:], w1.rearrange("(p j) m -> p (j m)", j=PACK))
-        for q in range(4):
-            nc.scalar.dma_start(
-                xs[32 * q : 32 * q + 4, :].bitcast(I32), x_scales[0, 4 * q : 4 * q + 4, :].bitcast(I32)
+        nc.sync.dma_start(table_words[:].bitcast(I32), x_words[0].rearrange("p n t -> p (n t)").bitcast(I32))
+        nc.sync.dma_start(stage, w1.rearrange("(p j) m -> p (j m)", j=PACK))
+        for quadrant in range(4):
+            nc.sync.dma_start(
+                table_scales[32 * quadrant : 32 * quadrant + 4, :].bitcast(I32),
+                x_scales[0, 4 * quadrant : 4 * quadrant + 4, :].bitcast(I32),
             )
         nc.sync.dma_start(up_t[:], up)
         nc.sync.dma_start(lo_t[:], lo)
 
-        nc.vector.memset(floor_in[:], -43.0)
-        nc.scalar.activation(floor[:], floor_in[:], ACT.Sigmoid)
+        floor_in = floats("floor_in", 1)
+        floor = floats("floor", 1)
+        nc.vector.memset(floor_in, -43.0)
+        nc.scalar.activation(floor, floor_in, ACT.Sigmoid)
 
-        pw = keep.tile([P, S], U32, name="pw", align_bytes=64)
-        ps = keep.tile([P, S], U8, name="ps", align_bytes=64)
-        nc.vector.tensor_copy(pw[:], xw[:].indirect(offs_t[:]))
-        nc.vector.tensor_copy(ps[:], xs[:].indirect(offs_t[:]))
+        picked_words = keep.tile([P, S], U32, name="picked_words", align_bytes=64)
+        picked_scales = keep.tile([P, S], U8, name="picked_scales", align_bytes=64)
+        nc.vector.tensor_copy(picked_words[:], table_words[:].indirect(offs_t[:]))
+        nc.vector.tensor_copy(picked_scales[:], table_scales[:].indirect(offs_t[:]))
 
-        spw = [keep.tile([P, 2 * S], F32, name=f"spw{t}") for t in range(TILES)]
-        sig1 = keep.tile([P, S], F32, name="sig1")
-        sig = [spw[1][:, S:], sig1[:]]
-        y = [psum.tile([P, S], F32, name=f"y{t}") for t in range(TILES)]
-        w_rows = stage[:].rearrange("p (j m) -> p j m", j=PACK)
-        for t in (1, 0):
+        soft_tile = [keep.tile([P, 2 * S], F32, name=f"soft{t}") for t in (LEAD, TRAIL)]
+        factor_tile = [keep.tile([P, 2 * S], F32, name=f"factor{t}") for t in (LEAD, TRAIL)]
+        soft = [tile[:, :S] for tile in soft_tile]
+        log_sig = [tile[:, S:] for tile in soft_tile]
+        factor = [tile[:, :S] for tile in factor_tile]
+        ratio = [tile[:, S:] for tile in factor_tile]
+        sig = [log_sig[TRAIL], floats("sig_trail")]
+
+        y = {(t, c): psum.tile([P, HALF], F32, name=f"y{t}_{c[0]}") for t in (LEAD, TRAIL) for c in HALVES}
+        w_rows = stage.rearrange("p (j m) -> p j m", j=PACK)
+        for t in (TRAIL, LEAD):
             w_bf = keep.tile([P, P, PACK], BF16, name=f"w_bf{t}", align_bytes=64)
-            w_codes = keep.tile([P, P], U32, name=f"w_codes{t}", align_bytes=64)
+            w_words = keep.tile([P, P], U32, name=f"w_words{t}", align_bytes=64)
             w_scales = keep.tile([P, P], U8, name=f"w_scales{t}", align_bytes=64)
             nc.scalar.copy(w_bf[:], w_rows[:, :, t * P : (t + 1) * P].rearrange("p j m -> p m j"))
             nc.vector.quantize_mx(
-                out=w_codes[:].bitcast(FP8X4), scales=w_scales[:], in_=w_bf[:].rearrange("p m j -> p (m j)")
+                out=w_words[:].bitcast(FP8X4), scales=w_scales[:], in_=w_bf[:].rearrange("p m j -> p (m j)")
             )
-            nc.tensor.matmul_mx(
-                out=y[t][:],
-                lhsT=w_codes[:].bitcast(FP8X4),
-                lhsT_scale=w_scales[:],
-                rhs=pw[:].bitcast(FP8X4),
-                rhs_scale=ps[:],
-                start=True,
-                stop=True,
-            )
-        for t in (1, 0):
-            nc.scalar.activation(sig[t], y[t][:], ACT.Sigmoid, scale=-1.0)
+            for c in HALVES:
+                nc.tensor.matmul_mx(
+                    out=y[t, c][:],
+                    lhsT=w_words[:].bitcast(FP8X4),
+                    lhsT_scale=w_scales[:],
+                    rhs=cols(picked_words, c).bitcast(FP8X4),
+                    rhs_scale=cols(picked_scales, c),
+                    start=True,
+                    stop=True,
+                )
+        for t in (TRAIL, LEAD):
+            for c in HALVES:
+                nc.scalar.activation(cols(sig[t], c), y[t, c][:], ACT.Sigmoid, scale=-1.0)
+
         one_t = stage[:, 0:S]
-        alpha_t = stage[:, S : S + TILES]
-        with nc.allow_non_contiguous_dma(reason="one alpha a partition"):
+        alpha_t = stage[:, S : S + 2]
+        with nc.allow_non_contiguous_dma(reason="alpha lies one value a partition and row tile"):
             nc.sync.dma_start(alpha_t, alpha.rearrange("(t p) o -> p (t o)", p=P))
         nc.sync.dma_start(one_t, one)
 
-        aw = [keep.tile([P, 2 * S], F32, name=f"aw{t}") for t in range(TILES)]
-        RS = ACT.Abs_reciprocal_sqrt
-        A, B, W = (0, HALF), (HALF, S), (0, S)
-        C, E = (256, 384), (384, 512)
+        shared_a = floats("shared_a", 2 * S + 3 * PIECE)
+        shared_b = floats("shared_b", 2 * S)
+        shared_c = floats("shared_c", S + HALF)
 
-        def buf(name, n=S):
-            return keep.tile([P, n], F32, name=name)[:]
+        def pair(name):
+            return [floats(f"{name}{t}") for t in (LEAD, TRAIL)]
 
-        def sl(ap, c, base=0):
-            return ap[:, base + c[0] : base + c[1]]
+        inv_root, sat, root_inv, gap2, gap4, factor_up, flux_scale, flux = [
+            pair(name) for name in ("inv_root", "sat", "root_inv", "gap2", "gap4", "factor_up", "flux_scale", "flux")
+        ]
+        suc2 = [shared_a[:, HALF : HALF + S], floats("suc2_trail")]
+        sat2 = [shared_a[:, S + 3 * PIECE :], floats("sat2_trail")]
+        neg_root = [shared_b[:, :S], floats("neg_root_trail")]
+        cond2 = {
+            (LEAD, FIRST): floats("cond2_lead", HALF),
+            (LEAD, SECOND): cols(shared_b, SECOND),
+            (TRAIL, FIRST): cols(shared_c, FIRST),
+            (TRAIL, SECOND): cols(shared_c, SECOND),
+        }
+        soft_up = [floats("soft_up_lead"), shared_a[:, S + PIECE : 2 * S + PIECE]]
+        drop = [shared_a[:, :S], shared_b[:, PIECE : PIECE + S]]
+        factors = [gap2[TRAIL], shared_b[:, S:]]
+        flux_root = [shared_c[:, HALF:], floats("flux_root_trail")]
 
-        def lst(tile, c):
-            return tile[:, c[0] // 16 : c[1] // 16]
+        def scalar_step(dst, src, func, **scale_bias):
+            def step(t, c):
+                nc.scalar.activation(cols(dst[t], c), cols(src[t], c), func, **scale_bias)
 
-        def act(dst, src, func, **kw):
-            nc.scalar.activation(dst, src, func, **kw)
+            return step
 
-        def f_ln(t, c):
-            act(sl(spw[t], c, S), sl(sig[t], c), ACT.Ln, bias=floor[:])
+        R = ACT.Abs_reciprocal_sqrt
+        take_log = scalar_step(log_sig, sig, ACT.Ln, bias=floor)
+        square_suction = scalar_step(suc2, soft, ACT.Square, bias=0.1)
+        square_sat = scalar_step(sat2, sat, ACT.Square)
+        invert_root = scalar_step(root_inv, sat2, R, bias=1.001, scale=-1.0)
+        square_gap = scalar_step(gap2, neg_root, ACT.Square, bias=1.0)
+        square_gap2 = scalar_step(gap4, gap2, ACT.Square)
+        add_one = scalar_step(factor, ratio, ACT.Identity, bias=1.0)
+        root_of_flux = scalar_step(flux_root, factors, R, bias=-12.5, scale=12.5)
+        square_flux_root = scalar_step(flux_scale, flux_root, ACT.Square)
 
-        def f_max(t, c):
-            nc.vector.scalar_tensor_tensor(sl(spw[t], c), sl(spw[t], c, S), -1.0, sl(y[t], c), ALU.mult, ALU.max)
+        def softplus(t, c):
+            nc.vector.scalar_tensor_tensor(cols(soft[t], c), cols(log_sig[t], c), -1.0, y[t, c][:], ALU.mult, ALU.max)
 
-        def f_q(t, c):
-            act(sl(q[t], c), sl(spw[t], c), ACT.Square, bias=0.1)
+        def retention(t, c):
+            nc.scalar.activation(cols(inv_root[t], c), cols(suc2[t], c), R, bias=1.0, scale=alpha_t[:, t : t + 1])
 
-        def f_rs(t, c):
-            act(sl(rs[t], c), sl(q[t], c), RS, bias=1.0, scale=alpha_t[:, t : t + 1])
+        def saturation(t, c):
+            nc.vector.tensor_tensor(cols(sat[t], c), cols(inv_root[t], c), cols(one_t, c), ALU.mult)
 
-        def f_sat(t, c):
-            nc.vector.tensor_tensor(sl(sat[t], c), sl(rs[t], c), sl(one_t, c), ALU.mult)
+        def negated_root(t, c):
+            nc.vector.scalar_tensor_tensor(
+                cols(neg_root[t], c), cols(sat2[t], c), -1.001, cols(root_inv[t], c), ALU.add, ALU.mult
+            )
 
-        def f_z(t, c):
-            act(sl(z[t], c), sl(sat[t], c), ACT.Square)
+        def square_cond(t, c):
+            nc.vector.tensor_tensor(cond2[t, c], cols(gap4[t], c), cols(sat[t], c), ALU.mult)
 
-        def f_rx(t, c):
-            act(sl(rx[t], c), sl(z[t], c), RS, bias=1.001, scale=-1.0)
+        def invert_cond(t, c):
+            nc.scalar.activation(cols(ratio[t], c), cond2[t, c], R, bias=1e-30, scale=1e4)
 
-        def f_nw(t, c):
-            nc.vector.scalar_tensor_tensor(sl(nw[t], c), sl(z[t], c), -1.001, sl(rx[t], c), ALU.add, ALU.mult)
+        def gather_soft_up(t, c):
+            nc.vector.tensor_copy(cols(soft_up[t], c), soft_tile[t][:].indirect(entries(up_t, c)))
 
-        def f_u2(t, c):
-            act(sl(u2[t], c), sl(nw[t], c), ACT.Square, bias=1.0)
+        def gather_drop(t, c):
+            lower = soft_tile[t][:].indirect(entries(lo_t, c))
+            nc.vector.tensor_tensor(cols(drop[t], c), lower, cols(soft_up[t], c), ALU.subtract)
 
-        def f_u4(t, c):
-            act(sl(u4[t], c), sl(u2[t], c), ACT.Square)
+        def gather_factor_up(t, c):
+            nc.vector.tensor_copy(cols(factor_up[t], c), factor_tile[t][:].indirect(entries(up_t, c)))
 
-        def f_c2(t, c):
-            nc.vector.tensor_tensor(sl(c2[t], c), sl(u4[t], c), sl(sat[t], c), ALU.mult)
+        def gather_factors(t, c):
+            lower = factor_tile[t][:].indirect(entries(lo_t, c))
+            nc.vector.tensor_tensor(cols(factors[t], c), lower, cols(factor_up[t], c), ALU.mult)
 
-        def f_a(t, c):
-            act(sl(aw[t], c, S), sl(c2[t], c), RS, bias=1e-30, scale=1e4)
+        def store_flux(t, c):
+            nc.vector.scalar_tensor_tensor(
+                cols(flux[t], c), cols(drop[t], c), 1.0, cols(flux_scale[t], c), ALU.add, ALU.mult
+            )
+            nc.sync.dma_start(out[t * P : (t + 1) * P, c[0] : c[1]], cols(flux[t], c))
 
-        def f_A(t, c):
-            act(sl(aw[t], c), sl(aw[t], c, S), ACT.Identity, bias=1.0)
+        def by_halves(t, *steps):
+            for step in steps:
+                for c in HALVES:
+                    step(t, c)
 
-        def f_su(t, c):
-            nc.vector.tensor_copy(sl(su[t], c), spw[t][:].indirect(lst(up_t, c)))
+        by_halves(LEAD, take_log)
+        by_halves(TRAIL, take_log)
+        by_halves(LEAD, softplus, square_suction)
+        gather_soft_up(LEAD, WHOLE)
+        by_halves(TRAIL, softplus)
 
-        def f_d(t, c):
-            nc.vector.tensor_tensor(sl(d[t], c), spw[t][:].indirect(lst(lo_t, c)), sl(su[t], c), ALU.subtract)
+        by_halves(LEAD, retention)
+        square_suction(TRAIL, WHOLE)
+        retention(TRAIL, WHOLE)
+        gather_drop(LEAD, FIRST)
+        by_halves(LEAD, saturation)
+        gather_drop(LEAD, SECOND)
+        gather_soft_up(TRAIL, (0, PIECE))
+        saturation(TRAIL, WHOLE)
 
-        def f_au(t, c):
-            nc.vector.tensor_copy(sl(au[t], c), aw[t][:].indirect(lst(up_t, c)))
+        by_halves(LEAD, square_sat, invert_root)
+        square_sat(TRAIL, WHOLE)
+        by_halves(LEAD, negated_root)
+        gather_soft_up(TRAIL, (PIECE, S))
 
-        def f_ab(t, c):
-            nc.vector.tensor_tensor(sl(ab[t], c), aw[t][:].indirect(lst(lo_t, c)), sl(au[t], c), ALU.mult)
+        square_gap(LEAD, FIRST)
+        gather_drop(TRAIL, (0, PIECE))
+        square_gap(LEAD, SECOND)
+        by_halves(LEAD, square_gap2)
+        invert_root(TRAIL, WHOLE)
+        by_halves(LEAD, square_cond)
+        negated_root(TRAIL, WHOLE)
 
-        def f_r(t, c):
-            act(sl(r[t], c), sl(ab[t], c), RS, bias=-12.5, scale=12.5)
+        by_halves(LEAD, invert_cond, add_one)
+        gather_drop(TRAIL, (PIECE, S - PIECE))
 
-        def f_r2(t, c):
-            act(sl(r2[t], c), sl(r[t], c), ACT.Square)
+        by_halves(TRAIL, square_gap, square_gap2)
+        gather_factor_up(LEAD, WHOLE)
+        by_halves(TRAIL, square_cond)
+        gather_factors(LEAD, WHOLE)
+        by_halves(TRAIL, invert_cond, add_one)
+        root_of_flux(LEAD, WHOLE)
+        square_flux_root(LEAD, WHOLE)
 
-        def f_o(t, c):
-            nc.vector.scalar_tensor_tensor(sl(o[t], c), sl(d[t], c), 1.0, sl(r2[t], c), ALU.add, ALU.mult)
-            nc.sync.dma_start(out[t * P : (t + 1) * P, c[0] : c[1]], sl(o[t], c))
-
-        rs, sat, nw, u4, ab, r, r2, o, z, q, rx, u2, c2, su, d, au = [[buf(f"{n}{t}") for t in range(TILES)] for n in ("rs", "sat", "nw", "u4", "ab", "r", "r2", "o", "z", "q", "rx", "u2", "c2", "su", "d", "au")]
-
-        t1 = buf("d0_q0_su1_z0", 1408)
-        d[0] = t1[:, 0:512]
-        q[0] = t1[:, 256:768]
-        su[1] = t1[:, 640:1152]
-        z[0] = t1[:, 896:1408]
-        t3 = buf("c20_d1_ab1", 1024)
-        c2[0] = t3[:, 0:512]
-        d[1] = t3[:, 256:768]
-        ab[1] = t3[:, 512:1024]
-        ab[0] = u2[1]
-        t5 = buf("c21_r0", 768)
-        c2[1] = t5[:, 0:512]
-        r[0] = t5[:, 256:768]
-
-        f_ln(0, A); f_ln(0, B); f_ln(1, A); f_ln(1, B)
-        f_max(0, A); f_max(0, B)
-        f_q(0, A); f_q(0, B)
-        f_su(0, W)
-        f_max(1, A); f_max(1, B)
-        f_rs(0, A); f_rs(0, B); f_q(1, W); f_rs(1, W)
-        f_d(0, A)
-        f_sat(0, A); f_sat(0, B)
-        f_d(0, B)
-        f_su(1, (0, 128))
-        f_sat(1, W)
-        f_z(0, A); f_z(0, B); f_rx(0, A); f_rx(0, B); f_z(1, W)
-        f_nw(0, A); f_nw(0, B)
-        f_su(1, (128, 512))
-        f_u2(0, A); f_u2(0, B); f_u4(0, A); f_u4(0, B); f_rx(1, W)
-        f_c2(0, A); f_c2(0, B)
-        f_nw(1, W)
-        f_a(0, A); f_a(0, B); f_A(0, A); f_A(0, B)
-        f_d(1, A)
-        f_u2(1, A); f_u2(1, B); f_u4(1, A); f_u4(1, B)
-        f_au(0, W)
-        f_c2(1, A); f_c2(1, B)
-        f_ab(0, W)
-        f_a(1, A); f_a(1, B); f_A(1, A); f_A(1, B)
-        f_r(0, W); f_r2(0, W)
-        f_au(1, A); f_au(1, B)
-        f_ab(1, A); f_ab(1, B)
-        f_o(0, W)
-        f_r(1, A); f_r2(1, A); f_r(1, B); f_r2(1, B)
-        f_d(1, B)
-        f_o(1, A); f_o(1, B)
+        by_halves(TRAIL, gather_factor_up, gather_factors)
+        store_flux(LEAD, WHOLE)
+        for c in HALVES:
+            root_of_flux(TRAIL, c)
+            square_flux_root(TRAIL, c)
+        gather_drop(TRAIL, (S - PIECE, S))
+        by_halves(TRAIL, store_flux)

@@ -55,7 +55,7 @@ def tile_picked_yrich_harm_p_kernel(
         nc.sync.dma_start(table_words[:].bitcast(I32), x_words[0].rearrange("p n t -> p (n t)").bitcast(I32))
         nc.sync.dma_start(stage, w1.rearrange("(p j) m -> p (j m)", j=PACK))
         for quadrant in range(4):
-            nc.sync.dma_start(
+            nc.scalar.dma_start(
                 table_scales[32 * quadrant : 32 * quadrant + 4, :].bitcast(I32),
                 x_scales[0, 4 * quadrant : 4 * quadrant + 4, :].bitcast(I32),
             )

@@ -23,7 +23,6 @@ FLOPS = 2 * K * N * S
 
 FIRST, SECOND, WHOLE = (0, HALF), (HALF, S), (0, S)
 HALVES = (FIRST, SECOND)
-PIECE = 128
 
 
 def tile_picked_yrich_harm_p_kernel(
@@ -80,7 +79,7 @@ def tile_picked_yrich_harm_p_kernel(
         ratio = [tile[:, S:] for tile in factor_tile]
         sig = [log_sig[TRAIL], floats("sig_trail")]
 
-        y = {(t, c): psum.tile([P, HALF], F32, name=f"y{t}_{c[0]}") for t in (LEAD, TRAIL) for c in HALVES}
+        y = [psum.tile([P, S], F32, name=f"y{t}") for t in (LEAD, TRAIL)]
         w_rows = stage.rearrange("p (j m) -> p j m", j=PACK)
         for t in (TRAIL, LEAD):
             w_bf = keep.tile([P, P, PACK], BF16, name=f"w_bf{t}", align_bytes=64)
@@ -90,19 +89,17 @@ def tile_picked_yrich_harm_p_kernel(
             nc.vector.quantize_mx(
                 out=w_words[:].bitcast(FP8X4), scales=w_scales[:], in_=w_bf[:].rearrange("p m j -> p (m j)")
             )
-            for c in HALVES:
-                nc.tensor.matmul_mx(
-                    out=y[t, c][:],
-                    lhsT=w_words[:].bitcast(FP8X4),
-                    lhsT_scale=w_scales[:],
-                    rhs=cols(picked_words, c).bitcast(FP8X4),
-                    rhs_scale=cols(picked_scales, c),
-                    start=True,
-                    stop=True,
-                )
+            nc.tensor.matmul_mx(
+                out=y[t][:],
+                lhsT=w_words[:].bitcast(FP8X4),
+                lhsT_scale=w_scales[:],
+                rhs=picked_words[:].bitcast(FP8X4),
+                rhs_scale=picked_scales[:],
+                start=True,
+                stop=True,
+            )
         for t in (TRAIL, LEAD):
-            for c in HALVES:
-                nc.scalar.activation(cols(sig[t], c), y[t, c][:], ACT.Sigmoid, scale=-1.0)
+            nc.scalar.activation(sig[t], y[t][:], ACT.Sigmoid, scale=-1.0)
 
         one_t = stage[:, 0:S]
         alpha_t = stage[:, S : S + 2]
@@ -110,29 +107,32 @@ def tile_picked_yrich_harm_p_kernel(
             nc.sync.dma_start(alpha_t, alpha.rearrange("(t p) o -> p (t o)", p=P))
         nc.sync.dma_start(one_t, one)
 
-        shared_a = floats("shared_a", 2 * S + 3 * PIECE)
-        shared_b = floats("shared_b", 2 * S)
-        shared_c = floats("shared_c", S + HALF)
-
         def pair(name):
             return [floats(f"{name}{t}") for t in (LEAD, TRAIL)]
 
-        inv_root, sat, root_inv, gap2, gap4, factor_up, flux_scale, flux = [
-            pair(name) for name in ("inv_root", "sat", "root_inv", "gap2", "gap4", "factor_up", "flux_scale", "flux")
+        def staggered(name, count):
+            tile = floats(name, S + (count - 1) * HALF)
+            return [tile[:, i * HALF : i * HALF + S] for i in range(count)]
+
+        inv_root, sat, sat2, neg_root = [pair(name) for name in ("inv_root", "sat", "sat2", "neg_root")]
+        gap2, gap4, factor_up, flux_scale, flux = [
+            pair(name) for name in ("gap2", "gap4", "factor_up", "flux_scale", "flux")
         ]
-        suc2 = [shared_a[:, HALF : HALF + S], floats("suc2_trail")]
-        sat2 = [shared_a[:, S + 3 * PIECE :], floats("sat2_trail")]
-        neg_root = [shared_b[:, :S], floats("neg_root_trail")]
+        suc2_lead, drop_lead, root_inv_lead = staggered("lead_chain", 3)
+        drop_trail, factors_trail = staggered("trail_faces", 2)
+        cond2_trail, flux_root_lead = staggered("hand_over", 2)
+        suc2 = [suc2_lead, floats("suc2_trail")]
+        root_inv = [root_inv_lead, floats("root_inv_trail")]
         cond2 = {
-            (LEAD, FIRST): floats("cond2_lead", HALF),
-            (LEAD, SECOND): cols(shared_b, SECOND),
-            (TRAIL, FIRST): cols(shared_c, FIRST),
-            (TRAIL, SECOND): cols(shared_c, SECOND),
+            (LEAD, FIRST): cols(sat2[LEAD], SECOND),
+            (LEAD, SECOND): cols(drop_trail, FIRST),
+            (TRAIL, FIRST): cols(cond2_trail, FIRST),
+            (TRAIL, SECOND): cols(cond2_trail, SECOND),
         }
-        soft_up = [floats("soft_up_lead"), shared_a[:, S + PIECE : 2 * S + PIECE]]
-        drop = [shared_a[:, :S], shared_b[:, PIECE : PIECE + S]]
-        factors = [gap2[TRAIL], shared_b[:, S:]]
-        flux_root = [shared_c[:, HALF:], floats("flux_root_trail")]
+        soft_up = [floats("soft_up_lead"), sat2[LEAD]]
+        drop = [drop_lead, drop_trail]
+        factors = [gap2[TRAIL], factors_trail]
+        flux_root = [flux_root_lead, floats("flux_root_trail")]
 
         def scalar_step(dst, src, func, **scale_bias):
             def step(t, c):
@@ -152,10 +152,19 @@ def tile_picked_yrich_harm_p_kernel(
         square_flux_root = scalar_step(flux_scale, flux_root, ACT.Square)
 
         def softplus(t, c):
-            nc.vector.scalar_tensor_tensor(cols(soft[t], c), cols(log_sig[t], c), -1.0, y[t, c][:], ALU.mult, ALU.max)
+            nc.vector.scalar_tensor_tensor(cols(soft[t], c), cols(log_sig[t], c), -1.0, cols(y[t], c), ALU.mult, ALU.max)
+
+        lead_bias = floats("lead_bias", 1)
+        nc.vector.tensor_scalar(lead_bias, alpha_t[:, LEAD : LEAD + 1], 0.01, 1.0, ALU.mult, ALU.add)
+        retention_bias = [lead_bias, 1.0]
+
+        def square_suction_on_vector(t, c):
+            nc.vector.scalar_tensor_tensor(cols(suc2[t], c), cols(soft[t], c), 0.2, cols(soft[t], c), ALU.add, ALU.mult)
 
         def retention(t, c):
-            nc.scalar.activation(cols(inv_root[t], c), cols(suc2[t], c), R, bias=1.0, scale=alpha_t[:, t : t + 1])
+            nc.scalar.activation(
+                cols(inv_root[t], c), cols(suc2[t], c), R, bias=retention_bias[t], scale=alpha_t[:, t : t + 1]
+            )
 
         def saturation(t, c):
             nc.vector.tensor_tensor(cols(sat[t], c), cols(inv_root[t], c), cols(one_t, c), ALU.mult)
@@ -198,34 +207,30 @@ def tile_picked_yrich_harm_p_kernel(
 
         by_halves(LEAD, take_log)
         by_halves(TRAIL, take_log)
-        by_halves(LEAD, softplus, square_suction)
-        gather_soft_up(LEAD, WHOLE)
+        by_halves(LEAD, softplus, square_suction_on_vector)
         by_halves(TRAIL, softplus)
+        gather_soft_up(LEAD, WHOLE)
 
         by_halves(LEAD, retention)
-        square_suction(TRAIL, WHOLE)
-        retention(TRAIL, WHOLE)
-        gather_drop(LEAD, FIRST)
+        by_halves(TRAIL, square_suction, retention)
         by_halves(LEAD, saturation)
-        gather_drop(LEAD, SECOND)
-        gather_soft_up(TRAIL, (0, PIECE))
+        gather_drop(LEAD, FIRST)
         saturation(TRAIL, WHOLE)
 
         by_halves(LEAD, square_sat, invert_root)
         square_sat(TRAIL, WHOLE)
         by_halves(LEAD, negated_root)
-        gather_soft_up(TRAIL, (PIECE, S))
+        gather_drop(LEAD, SECOND)
+        gather_soft_up(TRAIL, FIRST)
 
-        square_gap(LEAD, FIRST)
-        gather_drop(TRAIL, (0, PIECE))
-        square_gap(LEAD, SECOND)
-        by_halves(LEAD, square_gap2)
+        by_halves(LEAD, square_gap, square_gap2)
         invert_root(TRAIL, WHOLE)
         by_halves(LEAD, square_cond)
         negated_root(TRAIL, WHOLE)
 
         by_halves(LEAD, invert_cond, add_one)
-        gather_drop(TRAIL, (PIECE, S - PIECE))
+        gather_soft_up(TRAIL, SECOND)
+        gather_drop(TRAIL, FIRST)
 
         by_halves(TRAIL, square_gap, square_gap2)
         gather_factor_up(LEAD, WHOLE)
@@ -240,5 +245,5 @@ def tile_picked_yrich_harm_p_kernel(
         for c in HALVES:
             root_of_flux(TRAIL, c)
             square_flux_root(TRAIL, c)
-        gather_drop(TRAIL, (S - PIECE, S))
+        gather_drop(TRAIL, SECOND)
         by_halves(TRAIL, store_flux)

from contextlib import ExitStack

import concourse.mybir as mybir

F32 = mybir.dt.float32
BF16 = mybir.dt.bfloat16
U32 = mybir.dt.uint32
I32 = mybir.dt.int32
U16 = mybir.dt.uint16
U8 = mybir.dt.uint8
FP8X4 = mybir.dt.float8_e4m3fn_x4
ACT = mybir.ActivationFunctionType
ALU = mybir.AluOpType

P = 128
K, T, N = 512, 1024, 256
S = 512
PACK = 4
LIST_ROWS = 16
HALF = S // 2
LEAD, TRAIL = 0, 1
FLOPS = 2 * K * N * S

FIRST, SECOND, WHOLE = (0, HALF), (HALF, S), (0, S)
HALVES = (FIRST, SECOND)


def tile_picked_yrich_harm_p_kernel(
    tc, x_words, x_scales, w1, one, alpha, offs, up, lo, out
):
    nc = tc.nc
    with ExitStack() as ctx:
        keep = ctx.enter_context(tc.tile_pool(name="keep", bufs=1))
        psum = ctx.enter_context(tc.psum_pool(name="psum", bufs=1))

        def floats(name, width=S):
            return keep.tile([P, width], F32, name=name)[:]

        def cols(ap, c):
            return ap[:, c[0] : c[1]]

        def entries(list_tile, c):
            return list_tile[:, c[0] // LIST_ROWS : c[1] // LIST_ROWS]

        offs_t = keep.tile([P, S // LIST_ROWS], U16, name="offs_t")
        up_t = keep.tile([P, S // LIST_ROWS], U16, name="up_t")
        lo_t = keep.tile([P, S // LIST_ROWS], U16, name="lo_t")
        table_words = keep.tile([P, T], U32, name="table_words", align_bytes=64)
        table_scales = keep.tile([P, T], U8, name="table_scales", align_bytes=64)
        stage = floats("stage", PACK * N)

        nc.vector.memset(table_scales[:].bitcast(I32), 0)
        nc.sync.dma_start(offs_t[:], offs)
        nc.sync.dma_start(table_words[:].bitcast(I32), x_words[0].rearrange("p n t -> p (n t)").bitcast(I32))
        nc.sync.dma_start(stage, w1.rearrange("(p j) m -> p (j m)", j=PACK))
        for quadrant in range(4):
            nc.scalar.dma_start(
                table_scales[32 * quadrant : 32 * quadrant + 4, :].bitcast(I32),
                x_scales[0, 4 * quadrant : 4 * quadrant + 4, :].bitcast(I32),
            )
        nc.sync.dma_start(up_t[:], up)
        nc.sync.dma_start(lo_t[:], lo)

        floor_in = floats("floor_in", 1)
        floor = floats("floor", 1)
        nc.vector.memset(floor_in, -43.0)
        nc.scalar.activation(floor, floor_in, ACT.Sigmoid)

        picked_words = keep.tile([P, S], U32, name="picked_words", align_bytes=64)
        picked_scales = keep.tile([P, S], U8, name="picked_scales", align_bytes=64)
        nc.vector.tensor_copy(picked_words[:], table_words[:].indirect(offs_t[:]))
        nc.vector.tensor_copy(picked_scales[:], table_scales[:].indirect(offs_t[:]))

        soft_tile = [keep.tile([P, 2 * S], F32, name=f"soft{t}") for t in (LEAD, TRAIL)]
        factor_tile = [keep.tile([P, 2 * S], F32, name=f"factor{t}") for t in (LEAD, TRAIL)]
        soft = [tile[:, :S] for tile in soft_tile]
        log_sig = [tile[:, S:] for tile in soft_tile]
        factor = [tile[:, :S] for tile in factor_tile]
        ratio = [tile[:, S:] for tile in factor_tile]
        sig = [log_sig[TRAIL], floats("sig_trail")]

        y = [psum.tile([P, S], F32, name=f"y{t}") for t in (LEAD, TRAIL)]
        w_rows = stage.rearrange("p (j m) -> p j m", j=PACK)
        for t in (TRAIL, LEAD):
            w_bf = keep.tile([P, P, PACK], BF16, name=f"w_bf{t}", align_bytes=64)
            w_words = keep.tile([P, P], U32, name=f"w_words{t}", align_bytes=64)
            w_scales = keep.tile([P, P], U8, name=f"w_scales{t}", align_bytes=64)
            nc.scalar.copy(w_bf[:], w_rows[:, :, t * P : (t + 1) * P].rearrange("p j m -> p m j"))
            nc.vector.quantize_mx(
                out=w_words[:].bitcast(FP8X4), scales=w_scales[:], in_=w_bf[:].rearrange("p m j -> p (m j)")
            )
            nc.tensor.matmul_mx(
                out=y[t][:],
                lhsT=w_words[:].bitcast(FP8X4),
                lhsT_scale=w_scales[:],
                rhs=picked_words[:].bitcast(FP8X4),
                rhs_scale=picked_scales[:],
                start=True,
                stop=True,
            )
        for t in (TRAIL, LEAD):
            nc.scalar.activation(sig[t], y[t][:], ACT.Sigmoid, scale=-1.0)

        one_t = stage[:, 0:S]
        alpha_t = stage[:, S : S + 2]
        with nc.allow_non_contiguous_dma(reason="alpha lies one value a partition and row tile"):
            nc.sync.dma_start(alpha_t, alpha.rearrange("(t p) o -> p (t o)", p=P))
        nc.sync.dma_start(one_t, one)

        def pair(name):
            return [floats(f"{name}{t}") for t in (LEAD, TRAIL)]

        def staggered(name, count):
            tile = floats(name, S + (count - 1) * HALF)
            return [tile[:, i * HALF : i * HALF + S] for i in range(count)]

        inv_root, sat, sat2, neg_root = [pair(name) for name in ("inv_root", "sat", "sat2", "neg_root")]
        gap2, gap4, factor_up, flux_scale, flux = [
            pair(name) for name in ("gap2", "gap4", "factor_up", "flux_scale", "flux")
        ]
        suc2_lead, drop_lead, root_inv_lead = staggered("lead_chain", 3)
        drop_trail, factors_trail = staggered("trail_faces", 2)
        cond2_trail, flux_root_lead = staggered("hand_over", 2)
        suc2 = [suc2_lead, floats("suc2_trail")]
        root_inv = [root_inv_lead, floats("root_inv_trail")]
        cond2 = {
            (LEAD, FIRST): cols(sat2[LEAD], SECOND),
            (LEAD, SECOND): cols(drop_trail, FIRST),
            (TRAIL, FIRST): cols(cond2_trail, FIRST),
            (TRAIL, SECOND): cols(cond2_trail, SECOND),
        }
        soft_up = [floats("soft_up_lead"), sat2[LEAD]]
        drop = [drop_lead, drop_trail]
        factors = [gap2[TRAIL], factors_trail]
        flux_root = [flux_root_lead, floats("flux_root_trail")]

        def scalar_step(dst, src, func, **scale_bias):
            def step(t, c):
                nc.scalar.activation(cols(dst[t], c), cols(src[t], c), func, **scale_bias)

            return step

        R = ACT.Abs_reciprocal_sqrt
        take_log = scalar_step(log_sig, sig, ACT.Ln, bias=floor)
        square_suction = scalar_step(suc2, soft, ACT.Square, bias=0.1)
        square_sat = scalar_step(sat2, sat, ACT.Square)
        invert_root = scalar_step(root_inv, sat2, R, bias=1.001, scale=-1.0)
        square_gap = scalar_step(gap2, neg_root, ACT.Square, bias=1.0)
        square_gap2 = scalar_step(gap4, gap2, ACT.Square)
        add_one = scalar_step(factor, ratio, ACT.Identity, bias=1.0)
        root_of_flux = scalar_step(flux_root, factors, R, bias=-12.5, scale=12.5)
        square_flux_root = scalar_step(flux_scale, flux_root, ACT.Square)

        def softplus(t, c):
            nc.vector.scalar_tensor_tensor(cols(soft[t], c), cols(log_sig[t], c), -1.0, cols(y[t], c), ALU.mult, ALU.max)

        lead_bias = floats("lead_bias", 1)
        nc.vector.tensor_scalar(lead_bias, alpha_t[:, LEAD : LEAD + 1], 0.01, 1.0, ALU.mult, ALU.add)
        retention_bias = [lead_bias, 1.0]

        def square_suction_on_vector(t, c):
            nc.vector.scalar_tensor_tensor(cols(suc2[t], c), cols(soft[t], c), 0.2, cols(soft[t], c), ALU.add, ALU.mult)

        def retention(t, c):
            nc.scalar.activation(
                cols(inv_root[t], c), cols(suc2[t], c), R, bias=retention_bias[t], scale=alpha_t[:, t : t + 1]
            )

        def saturation(t, c):
            nc.vector.tensor_tensor(cols(sat[t], c), cols(inv_root[t], c), cols(one_t, c), ALU.mult)

        def negated_root(t, c):
            nc.vector.scalar_tensor_tensor(
                cols(neg_root[t], c), cols(sat2[t], c), -1.001, cols(root_inv[t], c), ALU.add, ALU.mult
            )

        def square_cond(t, c):
            nc.vector.tensor_tensor(cond2[t, c], cols(gap4[t], c), cols(sat[t], c), ALU.mult)

        def invert_cond(t, c):
            nc.scalar.activation(cols(ratio[t], c), cond2[t, c], R, bias=1e-30, scale=1e4)

        def gather_soft_up(t, c):
            nc.vector.tensor_copy(cols(soft_up[t], c), soft_tile[t][:].indirect(entries(up_t, c)))

        def gather_drop(t, c):
            lower = soft_tile[t][:].indirect(entries(lo_t, c))
            nc.vector.tensor_tensor(cols(drop[t], c), lower, cols(soft_up[t], c), ALU.subtract)

        def gather_factor_up(t, c):
            nc.vector.tensor_copy(cols(factor_up[t], c), factor_tile[t][:].indirect(entries(up_t, c)))

        def gather_factors(t, c):
            lower = factor_tile[t][:].indirect(entries(lo_t, c))
            nc.vector.tensor_tensor(cols(factors[t], c), lower, cols(factor_up[t], c), ALU.mult)

        def store_flux(t, c):
            nc.vector.scalar_tensor_tensor(
                cols(flux[t], c), cols(drop[t], c), 1.0, cols(flux_scale[t], c), ALU.add, ALU.mult
            )
            nc.sync.dma_start(out[t * P : (t + 1) * P, c[0] : c[1]], cols(flux[t], c))

        def by_halves(t, *steps):
            for step in steps:
                for c in HALVES:
                    step(t, c)

        by_halves(LEAD, take_log)
        by_halves(TRAIL, take_log)
        by_halves(LEAD, softplus, square_suction_on_vector)
        by_halves(TRAIL, softplus)
        gather_soft_up(LEAD, WHOLE)

        by_halves(LEAD, retention)
        by_halves(TRAIL, square_suction, retention)
        by_halves(LEAD, saturation)
        gather_drop(LEAD, FIRST)
        saturation(TRAIL, WHOLE)

        by_halves(LEAD, square_sat, invert_root)
        square_sat(TRAIL, WHOLE)
        by_halves(LEAD, negated_root)
        gather_drop(LEAD, SECOND)
        gather_soft_up(TRAIL, FIRST)

        by_halves(LEAD, square_gap, square_gap2)
        invert_root(TRAIL, WHOLE)
        by_halves(LEAD, square_cond)
        negated_root(TRAIL, WHOLE)

        by_halves(LEAD, invert_cond, add_one)
        gather_soft_up(TRAIL, SECOND)
        gather_drop(TRAIL, FIRST)

        by_halves(TRAIL, square_gap, square_gap2)
        gather_factor_up(LEAD, WHOLE)
        by_halves(TRAIL, square_cond)
        gather_factors(LEAD, WHOLE)
        by_halves(TRAIL, invert_cond, add_one)
        root_of_flux(LEAD, WHOLE)
        square_flux_root(LEAD, WHOLE)

        by_halves(TRAIL, gather_factor_up, gather_factors)
        store_flux(LEAD, WHOLE)
        for c in HALVES:
            root_of_flux(TRAIL, c)
            square_flux_root(TRAIL, c)
        gather_drop(TRAIL, SECOND)
        by_halves(TRAIL, store_flux)
